import numpy as np
import ml_dtypes


def mxq(x, axis, fmt="e4m3"):
    dtype, down = {"e4m3": (ml_dtypes.float8_e4m3fn, 7), "e5m2": (ml_dtypes.float8_e5m2, 14)}[fmt]
    v = np.moveaxis(np.asarray(x, np.float32).astype(ml_dtypes.bfloat16).astype(np.float64), axis, -1)
    blocks = v.reshape(v.shape[:-1] + (-1, 32))
    amax = np.abs(blocks).max(-1, keepdims=True)
    byte = np.maximum(np.where(amax > 0, np.frexp(amax)[1] - 1 + 127, 0) - down, 1)
    scale = np.exp2(byte - 127.0)
    codes = (blocks / scale).astype(np.float32).astype(dtype).astype(np.float64)
    return np.moveaxis((codes * scale).reshape(v.shape), -1, axis)


WIDE = False


def mx_kscale(k):
    if not WIDE:
        return np.ones(k)
    levels = np.array([10, -10, 5, -5, 0])
    if k % 512:
        return np.exp2(np.random.permutation(np.resize(levels, k // 32))).repeat(32)
    a = np.empty((k // 512, 16))
    for p in range(k // 512):
        a[p, :8] = np.random.permutation(np.resize(levels, 8))
        for g in range(8):
            far = levels[np.abs(levels - a[p, g]) >= 10]
            a[p, g + 8] = far[np.random.randint(len(far))]
    return np.exp2(a.ravel()).repeat(32)


def f64(x):
    return np.asarray(x).astype(np.float64)


def striped(idx):
    return np.tile(idx.reshape(-1, 16).T, (8, 1)).astype(np.uint16)


def unstriped(offs):
    return offs[:16].T.reshape(-1).astype(np.int64)


E2M1 = np.array([0.0, 0.5, 1.0, 1.5, 2.0, 3.0, 4.0, 6.0, -0.0, -0.5, -1.0, -1.5, -2.0, -3.0, -4.0, -6.0])


def pack_weight(w, fmt):
    k, n = w.shape
    w = f64(np.asarray(w, np.float32).astype(ml_dtypes.bfloat16)).reshape(k // 32, 32, n)
    amax = np.abs(w).max(1)
    if fmt == "e4m3":
        byte = np.frexp(amax)[1] - 1 + 127 - 7
    else:
        mant, ex = np.frexp(amax / 6.0)
        byte = np.where(mant > 0.5, ex, ex - 1) + 127
    byte = np.clip(np.where(amax > 0, byte, 1), 1, 254)
    scaled = (w * np.exp2(127.0 - byte)[:, None, :]).reshape(k, n).astype(np.float32)
    by_word = np.ascontiguousarray(scaled.reshape(k // 512, 128, 4, n).transpose(0, 1, 3, 2))
    if fmt == "e4m3":
        words = by_word.astype(ml_dtypes.float8_e4m3fn).view(np.uint8)
    else:
        c = by_word.astype(ml_dtypes.float4_e2m1fn).view(np.uint8) & 0xF
        words = (c[..., 0::2] | (c[..., 1::2] << 4)).reshape(k // 512, 128, 2 * n)
    return np.ascontiguousarray(words), np.ascontiguousarray(byte.astype(np.uint8).reshape(k // 512, 16, n))


def unpack_weight(words, scales, fmt):
    g, _, n = scales.shape
    words = np.ascontiguousarray(words).reshape(g, 128, n, -1)
    if fmt == "e4m3":
        vals = words.view(ml_dtypes.float8_e4m3fn).astype(np.float64)
    else:
        nib = np.empty((g, 128, n, 4), np.uint8)
        nib[..., 0::2] = words & 0xF
        nib[..., 1::2] = words >> 4
        vals = E2M1[nib]
    vals = vals * np.repeat(np.exp2(scales.astype(np.float64) - 127.0), 8, axis=1)[..., None]
    return vals.transpose(0, 1, 3, 2).reshape(g * 512, n)


def pack_table(v):
    words, scales = pack_weight(v, "e4m3")
    return np.concatenate([words.reshape(words.shape[0], -1), scales.reshape(scales.shape[0], -1)], axis=1)


def unpack_table(tab):
    g, t = tab.shape[0], tab.shape[1] // 528
    return unpack_weight(tab[:, :512 * t].reshape(g, 128, t, 4), tab[:, 512 * t:].reshape(g, 16, t), "e4m3")


def gelu(v):
    return 0.5 * v * (1.0 + np.tanh(np.sqrt(2.0 / np.pi) * (v + 0.044715 * v**3)))


K, M, T, S = 2048, 256, 512, 256


def setup_inputs():
    n = np.random.standard_normal
    s = mx_kscale(K)[:, None]
    p_w4 = pack_weight(n((K, M)) / np.sqrt(K) / s, "e2m1")
    return {
        "tab": pack_table(n((K, T)) * s),
        "w4_words": p_w4[0],
        "w4_scales": p_w4[1],
        "dw": (0.3 * n((K, M)) / np.sqrt(K) / s).astype(np.float32),
        "b": (0.3 * n(256)).astype(np.float32),
        "offs": striped(np.random.permutation(T)[:S]),
    }


def reference(tab, w4_words, w4_scales, dw, b, offs):
    tab_ = unpack_table(tab)[:, unstriped(offs)]
    w4_ = unpack_weight(w4_words, w4_scales, "e2m1")
    dw_ = mxq(f64(dw), 0, "e4m3")
    y = tab_.T @ w4_ + tab_.T @ dw_
    return gelu(y + f64(b)[None, :])

@@ -1,0 +1,181 @@
+from contextlib import ExitStack
+
+import concourse.mybir as mybir
+from concourse.masks import make_identity
+
+K, M, T, S = 2048, 256, 512, 256
+FLOPS = 2 * 2 * K * M * S
+
+F32 = mybir.dt.float32
+BF16 = mybir.dt.bfloat16
+I32 = mybir.dt.int32
+U32 = mybir.dt.uint32
+U16 = mybir.dt.uint16
+U8 = mybir.dt.uint8
+E4M3X4 = mybir.dt.float8_e4m3fn_x4
+E2M1X4 = mybir.dt.float4_e2m1fn_x4
+GELU = mybir.ActivationFunctionType.Gelu_apprx_tanh
+ADD = mybir.AluOpType.add
+
+P = 128
+PASSES = K // 512
+H = 128
+
+
+def tile_list_tabd_tm_gelu_kernel(tc, tab, w4_words, w4_scales, dw, b, offs, out):
+    nc = tc.nc
+    with ExitStack() as ctx:
+        keep = ctx.enter_context(tc.tile_pool(name="keep", bufs=1))
+        psum = ctx.enter_context(tc.psum_pool(name="psum", bufs=1))
+
+        offsets = keep.tile([P, S // 16], U16, name="offsets")
+        words = [keep.tile([P, T], I32, name=f"words{a}", align_bytes=64) for a in range(PASSES)]
+        table_scales = keep.tile([P, PASSES * T], U8, name="table_scales", align_bytes=64)
+        w4_codes = [keep.tile([P, 2, 2 * M], U8, name=f"w4_codes{g}", align_bytes=64) for g in range(PASSES // 2)]
+        w4_scale = keep.tile([P, PASSES * M], U8, name="w4_scale", align_bytes=64)
+        picked_words = [keep.tile([P, S], U32, name=f"picked_words{a}", align_bytes=64) for a in range(PASSES)]
+        picked_scales = [keep.tile([P, S], U8, name=f"picked_scales{a}", align_bytes=64) for a in range(PASSES)]
+        parts = [(a, 0, M) for a in range(PASSES - 1)] + [(PASSES - 1, 0, H), (PASSES - 1, H, H)]
+        raw = [keep.tile([P, 4, n], F32, name=f"raw{i}", align_bytes=64) for i, (a, c, n) in enumerate(parts)]
+        grouped = [keep.tile([P, 4 * n], BF16, name=f"grouped{i}", align_bytes=64) for i, (a, c, n) in enumerate(parts)]
+        dw_codes = [keep.tile([P, n], U32, name=f"dw_codes{i}", align_bytes=64) for i, (a, c, n) in enumerate(parts)]
+        dw_scales = [keep.tile([P, n], U8, name=f"dw_scales{i}", align_bytes=64) for i, (a, c, n) in enumerate(parts)]
+        bias_cols = keep.tile([P, 2], F32, name="bias_cols")
+        identity = keep.tile([P, P], F32, name="identity", align_bytes=64)
+        bias = keep.tile([P, M], F32, name="bias", align_bytes=64)
+        dummy = keep.tile([P, 1], F32, name="dummy")
+
+        bias_psum = psum.tile([P, M], F32, name="bias_psum")
+        acc = {(j, h): psum.tile([P, H], F32, name=f"acc{j}{h}") for h in range(2) for j in range(2)}
+
+        tab32 = tab.bitcast(I32)
+        table_words = T * P
+        tab_scale_rows = tab32[:, table_words:].rearrange("a (q t) -> q a t", q=16)
+        w4_scale_rows = w4_scales.bitcast(I32).rearrange("a q n -> q a n")
+
+        def load_words(a):
+            nc.sync.dma_start(words[a][:], tab32[a, 0:table_words].rearrange("(p t) -> p t", p=P))
+
+        def load_dw(i):
+            a, c, n = parts[i]
+            rows = dw[512 * a : 512 * (a + 1), c : c + n].rearrange("(p j) n -> p j n", j=4)
+            nc.sync.dma_start(raw[i][:], rows)
+
+        def load_w4(g):
+            nc.sync.dma_start(
+                w4_codes[g][:].bitcast(I32), w4_words.bitcast(I32)[2 * g : 2 * g + 2].rearrange("a p n -> p a n")
+            )
+
+        nc.vector.memset(dummy[:], 0.0)
+        nc.vector.memset(table_scales[:].bitcast(I32), 0)
+        nc.gpsimd.memset(w4_scale[:].bitcast(I32), 0)
+        nc.scalar.activation(dummy[:], dummy[:], GELU)
+
+        nc.sync.dma_start(offsets[:], offs)
+        load_words(0)
+        for q in range(4):
+            nc.sync.dma_start(
+                table_scales[32 * q : 32 * q + 4, :].bitcast(I32).rearrange("q (a t) -> q a t", a=PASSES),
+                tab_scale_rows[4 * q : 4 * q + 4],
+            )
+        for q in range(4):
+            nc.gpsimd.dma_start(
+                w4_scale[32 * q : 32 * q + 4, :].bitcast(I32).rearrange("q (a n) -> q a n", a=PASSES),
+                w4_scale_rows[4 * q : 4 * q + 4],
+            )
+        with nc.allow_non_contiguous_dma(reason="256 bias values, one to a partition"):
+            nc.gpsimd.dma_start(bias_cols[:], b.rearrange("(h p) -> p h", p=P))
+        load_words(1)
+        load_dw(0)
+        load_words(2)
+        load_dw(1)
+        load_words(3)
+        load_dw(2)
+        load_w4(0)
+        load_dw(3)
+        load_dw(4)
+        load_w4(1)
+
+        make_identity(nc, identity[:])
+        for h in range(2):
+            nc.tensor.transpose(
+                bias_psum[:, h * P : (h + 1) * P], bias_cols[:, h : h + 1].to_broadcast([P, P]), identity[:]
+            )
+        nc.scalar.copy(bias[:], bias_psum[:])
+
+        def gather(a):
+            nc.vector.tensor_copy(picked_words[a][:], words[a][:].bitcast(U32).indirect(offsets[:]))
+            nc.vector.tensor_copy(picked_scales[a][:], table_scales[:, a * T : (a + 1) * T].indirect(offsets[:]))
+
+        def interleave(copy, i, c0, c1):
+            dst = grouped[i][:, 4 * c0 : 4 * c1].rearrange("p (c i t) -> p c t i", i=4, t=4)
+            copy(dst, raw[i][:, :, c0:c1].rearrange("p t (c i) -> p c t i", i=4))
+
+        def quantize(i):
+            nc.vector.quantize_mx(out=dw_codes[i][:].bitcast(E4M3X4), scales=dw_scales[i][:], in_=grouped[i][:])
+
+        def table_operand(a, j):
+            cols = slice(j * H, (j + 1) * H)
+            return dict(lhsT=picked_words[a][:, cols].bitcast(E4M3X4), lhsT_scale=picked_scales[a][:, cols])
+
+        def multiply_w4(a):
+            for h in range(2):
+                for j in range(2):
+                    nc.tensor.matmul_mx(
+                        out=acc[j, h][:],
+                        **table_operand(a, j),
+                        rhs=w4_codes[a // 2][:, a % 2, 2 * H * h : 2 * H * (h + 1)].bitcast(E2M1X4),
+                        rhs_scale=w4_scale[:, a * M + H * h : a * M + H * (h + 1)],
+                        start=False,
+                        stop=False,
+                    )
+
+        def multiply_dw(i):
+            a, c, n = parts[i]
+            for c0 in range(0, n, H):
+                h = (c + c0) // H
+                for j in range(2):
+                    nc.tensor.matmul_mx(
+                        out=acc[j, h][:],
+                        **table_operand(a, j),
+                        rhs=dw_codes[i][:, c0 : c0 + H].bitcast(E4M3X4),
+                        rhs_scale=dw_scales[i][:, c0 : c0 + H],
+                        start=(a == 0),
+                        stop=(a == PASSES - 1),
+                    )
+
+        def finish(h):
+            cols = slice(h * H, (h + 1) * H)
+            for j in range(2):
+                biased = keep.tile([P, H], F32, name=f"biased{j}{h}", align_bytes=64)
+                result = keep.tile([P, H], F32, name=f"result{j}{h}", align_bytes=64)
+                nc.vector.tensor_tensor(biased[:], acc[j, h][:], bias[:, cols], ADD)
+                nc.scalar.activation(result[:], biased[:], GELU)
+                nc.sync.dma_start(out[j * H : (j + 1) * H, cols], result[:])
+
+        gather(0)
+        gather(1)
+        interleave(nc.scalar.copy, 0, 0, M)
+        gather(2)
+        quantize(0)
+        multiply_dw(0)
+        interleave(nc.scalar.copy, 1, 0, M)
+        gather(3)
+        quantize(1)
+        multiply_dw(1)
+        interleave(nc.scalar.copy, 2, 0, M)
+        quantize(2)
+        multiply_dw(2)
+        multiply_w4(0)
+        multiply_w4(1)
+        interleave(nc.vector.tensor_copy, 3, 0, H)
+        interleave(nc.vector.tensor_copy, 4, 0, 80)
+        interleave(nc.scalar.copy, 4, 80, H)
+        quantize(3)
+        quantize(4)
+        multiply_w4(2)
+        multiply_w4(3)
+        multiply_dw(3)
+        finish(0)
+        multiply_dw(4)
+        finish(1)

@@ -31,118 +31,119 @@ def tile_list_tabd_tm_gelu_kernel(tc, tab, w4_words, w4_scales, dw, b, offs, out
         offsets = keep.tile([P, S // 16], U16, name="offsets")
         words = [keep.tile([P, T], I32, name=f"words{a}", align_bytes=64) for a in range(PASSES)]
         table_scales = keep.tile([P, PASSES * T], U8, name="table_scales", align_bytes=64)
-        w4_codes = [keep.tile([P, 2, 2 * M], U8, name=f"w4_codes{g}", align_bytes=64) for g in range(PASSES // 2)]
+        w4_parts = [(0, 3), (3, 1)]
+        w4_codes = [keep.tile([P, n, 2 * M], U8, name=f"w4_codes{g}", align_bytes=64) for g, (a, n) in enumerate(w4_parts)]
         w4_scale = keep.tile([P, PASSES * M], U8, name="w4_scale", align_bytes=64)
         picked_words = [keep.tile([P, S], U32, name=f"picked_words{a}", align_bytes=64) for a in range(PASSES)]
         picked_scales = [keep.tile([P, S], U8, name=f"picked_scales{a}", align_bytes=64) for a in range(PASSES)]
-        parts = [(a, 0, M) for a in range(PASSES - 1)] + [(PASSES - 1, 0, H), (PASSES - 1, H, H)]
-        raw = [keep.tile([P, 4, n], F32, name=f"raw{i}", align_bytes=64) for i, (a, c, n) in enumerate(parts)]
-        grouped = [keep.tile([P, 4 * n], BF16, name=f"grouped{i}", align_bytes=64) for i, (a, c, n) in enumerate(parts)]
-        dw_codes = [keep.tile([P, n], U32, name=f"dw_codes{i}", align_bytes=64) for i, (a, c, n) in enumerate(parts)]
-        dw_scales = [keep.tile([P, n], U8, name=f"dw_scales{i}", align_bytes=64) for i, (a, c, n) in enumerate(parts)]
+        parts = [(a, 0, 4) for a in range(PASSES - 1)] + [(PASSES - 1, 0, 2), (PASSES - 1, 2, 2)]
+        raw = [keep.tile([P, rows, M], F32, name=f"raw{i}", align_bytes=64) for i, (a, t, rows) in enumerate(parts)]
+        grouped = [keep.tile([P, 4 * M], BF16, name=f"grouped{a}", align_bytes=64) for a in range(PASSES)]
+        dw_codes = [keep.tile([P, M], U32, name=f"dw_codes{a}", align_bytes=64) for a in range(PASSES)]
+        dw_scales = [keep.tile([P, M], U8, name=f"dw_scales{a}", align_bytes=64) for a in range(PASSES)]
+        bias_rows = keep.tile([P, P], F32, name="bias_rows", align_bytes=64)
         bias_cols = keep.tile([P, 2], F32, name="bias_cols")
         identity = keep.tile([P, P], F32, name="identity", align_bytes=64)
         bias = keep.tile([P, M], F32, name="bias", align_bytes=64)
         dummy = keep.tile([P, 1], F32, name="dummy")
 
+        bias_cols_psum = psum.tile([P, P], F32, name="bias_cols_psum")
         bias_psum = psum.tile([P, M], F32, name="bias_psum")
         acc = {(j, h): psum.tile([P, H], F32, name=f"acc{j}{h}") for h in range(2) for j in range(2)}
 
         tab32 = tab.bitcast(I32)
         table_words = T * P
-        tab_scale_rows = tab32[:, table_words:].rearrange("a (q t) -> q a t", q=16)
-        w4_scale_rows = w4_scales.bitcast(I32).rearrange("a q n -> q a n")
+        tab_scale_rows = tab32[:, table_words:].rearrange("a (q r t) -> r q a t", q=4, r=4)
+        w4_scale_rows = w4_scales.bitcast(I32).rearrange("a (q r) n -> r q a n", q=4)
 
         def load_words(a):
             nc.sync.dma_start(words[a][:], tab32[a, 0:table_words].rearrange("(p t) -> p t", p=P))
 
         def load_dw(i):
-            a, c, n = parts[i]
-            rows = dw[512 * a : 512 * (a + 1), c : c + n].rearrange("(p j) n -> p j n", j=4)
-            nc.sync.dma_start(raw[i][:], rows)
+            a, t, rows = parts[i]
+            nc.sync.dma_start(
+                raw[i][:], dw[512 * a : 512 * (a + 1), :].rearrange("(p j) n -> p j n", j=4)[:, t : t + rows, :]
+            )
 
         def load_w4(g):
-            nc.sync.dma_start(
-                w4_codes[g][:].bitcast(I32), w4_words.bitcast(I32)[2 * g : 2 * g + 2].rearrange("a p n -> p a n")
-            )
+            a, n = w4_parts[g]
+            nc.sync.dma_start(w4_codes[g][:].bitcast(I32), w4_words.bitcast(I32)[a : a + n].rearrange("a p n -> p a n"))
 
         nc.vector.memset(dummy[:], 0.0)
         nc.vector.memset(table_scales[:].bitcast(I32), 0)
-        nc.gpsimd.memset(w4_scale[:].bitcast(I32), 0)
+        nc.vector.memset(w4_scale[:].bitcast(I32), 0)
+        nc.vector.memset(bias_rows[:], 0.0)
+        make_identity(nc, identity[:])
         nc.scalar.activation(dummy[:], dummy[:], GELU)
 
         nc.sync.dma_start(offsets[:], offs)
         load_words(0)
-        for q in range(4):
-            nc.sync.dma_start(
-                table_scales[32 * q : 32 * q + 4, :].bitcast(I32).rearrange("q (a t) -> q a t", a=PASSES),
-                tab_scale_rows[4 * q : 4 * q + 4],
-            )
-        for q in range(4):
-            nc.gpsimd.dma_start(
-                w4_scale[32 * q : 32 * q + 4, :].bitcast(I32).rearrange("q (a n) -> q a n", a=PASSES),
-                w4_scale_rows[4 * q : 4 * q + 4],
-            )
-        with nc.allow_non_contiguous_dma(reason="256 bias values, one to a partition"):
-            nc.gpsimd.dma_start(bias_cols[:], b.rearrange("(h p) -> p h", p=P))
         load_words(1)
+        for r in range(4):
+            nc.sync.dma_start(
+                table_scales[r:P:32, :].bitcast(I32).rearrange("q (a t) -> q a t", a=PASSES), tab_scale_rows[r]
+            )
         load_dw(0)
         load_words(2)
+        for r in range(4):
+            nc.sync.dma_start(
+                w4_scale[r:P:32, :].bitcast(I32).rearrange("q (a n) -> q a n", a=PASSES), w4_scale_rows[r]
+            )
+        load_w4(0)
         load_dw(1)
+        nc.sync.dma_start(bias_rows[0:2, :], b.rearrange("(h n) -> h n", h=2))
         load_words(3)
         load_dw(2)
-        load_w4(0)
         load_dw(3)
         load_dw(4)
         load_w4(1)
 
-        make_identity(nc, identity[:])
-        for h in range(2):
-            nc.tensor.transpose(
-                bias_psum[:, h * P : (h + 1) * P], bias_cols[:, h : h + 1].to_broadcast([P, P]), identity[:]
-            )
-        nc.scalar.copy(bias[:], bias_psum[:])
-
-        def gather(a):
+        def gather_words(a):
             nc.vector.tensor_copy(picked_words[a][:], words[a][:].bitcast(U32).indirect(offsets[:]))
+
+        def gather_scales(a):
             nc.vector.tensor_copy(picked_scales[a][:], table_scales[:, a * T : (a + 1) * T].indirect(offsets[:]))
 
         def interleave(copy, i, c0, c1):
-            dst = grouped[i][:, 4 * c0 : 4 * c1].rearrange("p (c i t) -> p c t i", i=4, t=4)
+            a, t, rows = parts[i]
+            dst = grouped[a][:, 4 * c0 : 4 * c1].rearrange("p (c i t) -> p c t i", i=4, t=4)[:, :, t : t + rows, :]
             copy(dst, raw[i][:, :, c0:c1].rearrange("p t (c i) -> p c t i", i=4))
 
-        def quantize(i):
-            nc.vector.quantize_mx(out=dw_codes[i][:].bitcast(E4M3X4), scales=dw_scales[i][:], in_=grouped[i][:])
+        def quantize(a, c0, c1):
+            nc.vector.quantize_mx(
+                out=dw_codes[a][:, c0:c1].bitcast(E4M3X4),
+                scales=dw_scales[a][:, c0:c1],
+                in_=grouped[a][:, 4 * c0 : 4 * c1],
+            )
 
         def table_operand(a, j):
             cols = slice(j * H, (j + 1) * H)
             return dict(lhsT=picked_words[a][:, cols].bitcast(E4M3X4), lhsT_scale=picked_scales[a][:, cols])
 
         def multiply_w4(a):
+            g = a // 3
             for h in range(2):
                 for j in range(2):
                     nc.tensor.matmul_mx(
                         out=acc[j, h][:],
                         **table_operand(a, j),
-                        rhs=w4_codes[a // 2][:, a % 2, 2 * H * h : 2 * H * (h + 1)].bitcast(E2M1X4),
+                        rhs=w4_codes[g][:, a % 3, 2 * H * h : 2 * H * (h + 1)].bitcast(E2M1X4),
                         rhs_scale=w4_scale[:, a * M + H * h : a * M + H * (h + 1)],
-                        start=False,
+                        start=(a == 0),
                         stop=False,
                     )
 
-        def multiply_dw(i):
-            a, c, n = parts[i]
-            for c0 in range(0, n, H):
-                h = (c + c0) // H
-                for j in range(2):
-                    nc.tensor.matmul_mx(
-                        out=acc[j, h][:],
-                        **table_operand(a, j),
-                        rhs=dw_codes[i][:, c0 : c0 + H].bitcast(E4M3X4),
-                        rhs_scale=dw_scales[i][:, c0 : c0 + H],
-                        start=(a == 0),
-                        stop=(a == PASSES - 1),
-                    )
+        def multiply_dw(a, h):
+            cols = slice(H * h, H * (h + 1))
+            for j in range(2):
+                nc.tensor.matmul_mx(
+                    out=acc[j, h][:],
+                    **table_operand(a, j),
+                    rhs=dw_codes[a][:, cols].bitcast(E4M3X4),
+                    rhs_scale=dw_scales[a][:, cols],
+                    start=False,
+                    stop=(a == PASSES - 1),
+                )
 
         def finish(h):
             cols = slice(h * H, (h + 1) * H)
@@ -153,29 +154,46 @@ def tile_list_tabd_tm_gelu_kernel(tc, tab, w4_words, w4_scales, dw, b, offs, out
                 nc.scalar.activation(result[:], biased[:], GELU)
                 nc.sync.dma_start(out[j * H : (j + 1) * H, cols], result[:])
 
-        gather(0)
-        gather(1)
+        gather_words(0)
+        gather_words(1)
+        gather_scales(0)
+        gather_scales(1)
         interleave(nc.scalar.copy, 0, 0, M)
-        gather(2)
-        quantize(0)
-        multiply_dw(0)
-        interleave(nc.scalar.copy, 1, 0, M)
-        gather(3)
-        quantize(1)
-        multiply_dw(1)
-        interleave(nc.scalar.copy, 2, 0, M)
-        quantize(2)
-        multiply_dw(2)
         multiply_w4(0)
         multiply_w4(1)
-        interleave(nc.vector.tensor_copy, 3, 0, H)
-        interleave(nc.vector.tensor_copy, 4, 0, 80)
-        interleave(nc.scalar.copy, 4, 80, H)
-        quantize(3)
-        quantize(4)
+        gather_words(2)
+        gather_scales(2)
+        quantize(0, 0, M)
+        multiply_dw(0, 0)
+        multiply_dw(0, 1)
         multiply_w4(2)
+        interleave(nc.scalar.copy, 1, 0, M)
+        gather_words(3)
+        gather_scales(3)
+        quantize(1, 0, M)
+        multiply_dw(1, 0)
+        multiply_dw(1, 1)
+
+        nc.tensor.transpose(bias_cols_psum[:], bias_rows[:], identity[:])
+        nc.scalar.copy(bias_cols[:], bias_cols_psum[:, 0:2])
+        for h in range(2):
+            nc.tensor.transpose(
+                bias_psum[:, h * P : (h + 1) * P], bias_cols[:, h : h + 1].to_broadcast([P, P]), identity[:]
+            )
+        nc.scalar.copy(bias[:], bias_psum[:])
+
+        interleave(nc.scalar.copy, 2, 96, M)
+        interleave(nc.vector.tensor_copy, 2, 0, 96)
+        quantize(2, 0, M)
+        multiply_dw(2, 0)
+        multiply_dw(2, 1)
+        interleave(nc.vector.tensor_copy, 3, 0, M)
+        interleave(nc.scalar.copy, 4, 0, H)
+        interleave(nc.vector.tensor_copy, 4, H, M)
         multiply_w4(3)
-        multiply_dw(3)
+        quantize(3, 0, H)
+        multiply_dw(3, 0)
+        quantize(3, H, M)
+        multiply_dw(3, 1)
         finish(0)
-        multiply_dw(4)
         finish(1)

@@ -70,30 +70,30 @@ def tile_list_tabd_tm_gelu_kernel(tc, tab, w4_words, w4_scales, dw, b, offs, out
             nc.sync.dma_start(w4_codes[g][:].bitcast(I32), w4_words.bitcast(I32)[a : a + n].rearrange("a p n -> p a n"))
 
         nc.vector.memset(dummy[:], 0.0)
+        nc.gpsimd.memset(bias_rows[:], 0.0)
         nc.vector.memset(table_scales[:].bitcast(I32), 0)
         nc.vector.memset(w4_scale[:].bitcast(I32), 0)
-        nc.vector.memset(bias_rows[:], 0.0)
-        make_identity(nc, identity[:])
         nc.scalar.activation(dummy[:], dummy[:], GELU)
 
+        nc.gpsimd.dma_start(bias_rows[0:2, :], b.rearrange("(h n) -> h n", h=2))
+        make_identity(nc, identity[:])
         nc.sync.dma_start(offsets[:], offs)
         load_words(0)
         load_words(1)
+        load_dw(0)
         for r in range(4):
             nc.sync.dma_start(
                 table_scales[r:P:32, :].bitcast(I32).rearrange("q (a t) -> q a t", a=PASSES), tab_scale_rows[r]
             )
-        load_dw(0)
+        load_dw(1)
         load_words(2)
+        load_dw(2)
+        load_words(3)
         for r in range(4):
             nc.sync.dma_start(
                 w4_scale[r:P:32, :].bitcast(I32).rearrange("q (a n) -> q a n", a=PASSES), w4_scale_rows[r]
             )
         load_w4(0)
-        load_dw(1)
-        nc.sync.dma_start(bias_rows[0:2, :], b.rearrange("(h n) -> h n", h=2))
-        load_words(3)
-        load_dw(2)
         load_dw(3)
         load_dw(4)
         load_w4(1)
@@ -129,7 +129,7 @@ def tile_list_tabd_tm_gelu_kernel(tc, tab, w4_words, w4_scales, dw, b, offs, out
                         **table_operand(a, j),
                         rhs=w4_codes[g][:, a % 3, 2 * H * h : 2 * H * (h + 1)].bitcast(E2M1X4),
                         rhs_scale=w4_scale[:, a * M + H * h : a * M + H * (h + 1)],
-                        start=(a == 0),
+                        start=False,
                         stop=False,
                     )
 
@@ -141,7 +141,7 @@ def tile_list_tabd_tm_gelu_kernel(tc, tab, w4_words, w4_scales, dw, b, offs, out
                     **table_operand(a, j),
                     rhs=dw_codes[a][:, cols].bitcast(E4M3X4),
                     rhs_scale=dw_scales[a][:, cols],
-                    start=False,
+                    start=(a == 0),
                     stop=(a == PASSES - 1),
                 )
 
@@ -154,26 +154,6 @@ def tile_list_tabd_tm_gelu_kernel(tc, tab, w4_words, w4_scales, dw, b, offs, out
                 nc.scalar.activation(result[:], biased[:], GELU)
                 nc.sync.dma_start(out[j * H : (j + 1) * H, cols], result[:])
 
-        gather_words(0)
-        gather_words(1)
-        gather_scales(0)
-        gather_scales(1)
-        interleave(nc.scalar.copy, 0, 0, M)
-        multiply_w4(0)
-        multiply_w4(1)
-        gather_words(2)
-        gather_scales(2)
-        quantize(0, 0, M)
-        multiply_dw(0, 0)
-        multiply_dw(0, 1)
-        multiply_w4(2)
-        interleave(nc.scalar.copy, 1, 0, M)
-        gather_words(3)
-        gather_scales(3)
-        quantize(1, 0, M)
-        multiply_dw(1, 0)
-        multiply_dw(1, 1)
-
         nc.tensor.transpose(bias_cols_psum[:], bias_rows[:], identity[:])
         nc.scalar.copy(bias_cols[:], bias_cols_psum[:, 0:2])
         for h in range(2):
@@ -182,12 +162,32 @@ def tile_list_tabd_tm_gelu_kernel(tc, tab, w4_words, w4_scales, dw, b, offs, out
             )
         nc.scalar.copy(bias[:], bias_psum[:])
 
-        interleave(nc.scalar.copy, 2, 96, M)
-        interleave(nc.vector.tensor_copy, 2, 0, 96)
+        gather_words(0)
+        gather_words(1)
+        gather_scales(0)
+        gather_scales(1)
+        interleave(nc.scalar.copy, 0, 0, M)
+        quantize(0, 0, M)
+        multiply_dw(0, 0)
+        multiply_dw(0, 1)
+        gather_words(2)
+        gather_scales(2)
+        interleave(nc.scalar.copy, 1, 0, M)
+        quantize(1, 0, M)
+        multiply_dw(1, 0)
+        multiply_dw(1, 1)
+        multiply_w4(0)
+        multiply_w4(1)
+        multiply_w4(2)
+        gather_words(3)
+        gather_scales(3)
+
+
+        interleave(nc.scalar.copy, 2, 0, M)
         quantize(2, 0, M)
         multiply_dw(2, 0)
         multiply_dw(2, 1)
-        interleave(nc.vector.tensor_copy, 3, 0, M)
+        interleave(nc.scalar.copy, 3, 0, M)
         interleave(nc.scalar.copy, 4, 0, H)
         interleave(nc.vector.tensor_copy, 4, H, M)
         multiply_w4(3)

@@ -31,8 +31,7 @@ def tile_list_tabd_tm_gelu_kernel(tc, tab, w4_words, w4_scales, dw, b, offs, out
         offsets = keep.tile([P, S // 16], U16, name="offsets")
         words = [keep.tile([P, T], I32, name=f"words{a}", align_bytes=64) for a in range(PASSES)]
         table_scales = keep.tile([P, PASSES * T], U8, name="table_scales", align_bytes=64)
-        w4_parts = [(0, 3), (3, 1)]
-        w4_codes = [keep.tile([P, n, 2 * M], U8, name=f"w4_codes{g}", align_bytes=64) for g, (a, n) in enumerate(w4_parts)]
+        w4_codes = keep.tile([P, PASSES, 2 * M], U8, name="w4_codes", align_bytes=64)
         w4_scale = keep.tile([P, PASSES * M], U8, name="w4_scale", align_bytes=64)
         picked_words = [keep.tile([P, S], U32, name=f"picked_words{a}", align_bytes=64) for a in range(PASSES)]
         picked_scales = [keep.tile([P, S], U8, name=f"picked_scales{a}", align_bytes=64) for a in range(PASSES)]
@@ -65,38 +64,33 @@ def tile_list_tabd_tm_gelu_kernel(tc, tab, w4_words, w4_scales, dw, b, offs, out
                 raw[i][:], dw[512 * a : 512 * (a + 1), :].rearrange("(p j) n -> p j n", j=4)[:, t : t + rows, :]
             )
 
-        def load_w4(g):
-            a, n = w4_parts[g]
-            nc.sync.dma_start(w4_codes[g][:].bitcast(I32), w4_words.bitcast(I32)[a : a + n].rearrange("a p n -> p a n"))
-
+        nc.gpsimd.memset(table_scales[:].bitcast(I32), 0)
+        nc.vector.memset(bias_rows[:], 0.0)
         nc.vector.memset(dummy[:], 0.0)
-        nc.gpsimd.memset(bias_rows[:], 0.0)
-        nc.vector.memset(table_scales[:].bitcast(I32), 0)
         nc.vector.memset(w4_scale[:].bitcast(I32), 0)
         nc.scalar.activation(dummy[:], dummy[:], GELU)
 
         nc.gpsimd.dma_start(bias_rows[0:2, :], b.rearrange("(h n) -> h n", h=2))
+        nc.gpsimd.dma_start(w4_codes[:].bitcast(I32), w4_words.bitcast(I32).rearrange("a p n -> p a n"))
         make_identity(nc, identity[:])
         nc.sync.dma_start(offsets[:], offs)
         load_words(0)
         load_words(1)
-        load_dw(0)
         for r in range(4):
             nc.sync.dma_start(
                 table_scales[r:P:32, :].bitcast(I32).rearrange("q (a t) -> q a t", a=PASSES), tab_scale_rows[r]
             )
+        load_dw(0)
         load_dw(1)
         load_words(2)
         load_dw(2)
-        load_words(3)
         for r in range(4):
             nc.sync.dma_start(
                 w4_scale[r:P:32, :].bitcast(I32).rearrange("q (a n) -> q a n", a=PASSES), w4_scale_rows[r]
             )
-        load_w4(0)
+        load_words(3)
         load_dw(3)
         load_dw(4)
-        load_w4(1)
 
         def gather_words(a):
             nc.vector.tensor_copy(picked_words[a][:], words[a][:].bitcast(U32).indirect(offsets[:]))
@@ -121,13 +115,12 @@ def tile_list_tabd_tm_gelu_kernel(tc, tab, w4_words, w4_scales, dw, b, offs, out
             return dict(lhsT=picked_words[a][:, cols].bitcast(E4M3X4), lhsT_scale=picked_scales[a][:, cols])
 
         def multiply_w4(a):
-            g = a // 3
             for h in range(2):
                 for j in range(2):
                     nc.tensor.matmul_mx(
                         out=acc[j, h][:],
                         **table_operand(a, j),
-                        rhs=w4_codes[g][:, a % 3, 2 * H * h : 2 * H * (h + 1)].bitcast(E2M1X4),
+                        rhs=w4_codes[:, a, 2 * H * h : 2 * H * (h + 1)].bitcast(E2M1X4),
                         rhs_scale=w4_scale[:, a * M + H * h : a * M + H * (h + 1)],
                         start=False,
                         stop=False,
@@ -170,27 +163,25 @@ def tile_list_tabd_tm_gelu_kernel(tc, tab, w4_words, w4_scales, dw, b, offs, out
         quantize(0, 0, M)
         multiply_dw(0, 0)
         multiply_dw(0, 1)
+        multiply_w4(0)
+        multiply_w4(1)
         gather_words(2)
         gather_scales(2)
         interleave(nc.scalar.copy, 1, 0, M)
         quantize(1, 0, M)
         multiply_dw(1, 0)
         multiply_dw(1, 1)
-        multiply_w4(0)
-        multiply_w4(1)
         multiply_w4(2)
         gather_words(3)
         gather_scales(3)
-
-
         interleave(nc.scalar.copy, 2, 0, M)
         quantize(2, 0, M)
         multiply_dw(2, 0)
         multiply_dw(2, 1)
+        multiply_w4(3)
         interleave(nc.scalar.copy, 3, 0, M)
         interleave(nc.scalar.copy, 4, 0, H)
         interleave(nc.vector.tensor_copy, 4, H, M)
-        multiply_w4(3)
         quantize(3, 0, H)
         multiply_dw(3, 0)
         quantize(3, H, M)

@@ -71,7 +71,6 @@ def tile_list_tabd_tm_gelu_kernel(tc, tab, w4_words, w4_scales, dw, b, offs, out
         nc.scalar.activation(dummy[:], dummy[:], GELU)
 
         nc.gpsimd.dma_start(bias_rows[0:2, :], b.rearrange("(h n) -> h n", h=2))
-        nc.gpsimd.dma_start(w4_codes[:].bitcast(I32), w4_words.bitcast(I32).rearrange("a p n -> p a n"))
         make_identity(nc, identity[:])
         nc.sync.dma_start(offsets[:], offs)
         load_words(0)
@@ -83,12 +82,13 @@ def tile_list_tabd_tm_gelu_kernel(tc, tab, w4_words, w4_scales, dw, b, offs, out
         load_dw(0)
         load_dw(1)
         load_words(2)
-        load_dw(2)
+        nc.sync.dma_start(w4_codes[:].bitcast(I32), w4_words.bitcast(I32).rearrange("a p n -> p a n"))
         for r in range(4):
             nc.sync.dma_start(
                 w4_scale[r:P:32, :].bitcast(I32).rearrange("q (a n) -> q a n", a=PASSES), w4_scale_rows[r]
             )
         load_words(3)
+        load_dw(2)
         load_dw(3)
         load_dw(4)
 
@@ -174,7 +174,8 @@ def tile_list_tabd_tm_gelu_kernel(tc, tab, w4_words, w4_scales, dw, b, offs, out
         multiply_w4(2)
         gather_words(3)
         gather_scales(3)
-        interleave(nc.scalar.copy, 2, 0, M)
+        interleave(nc.scalar.copy, 2, 0, H)
+        interleave(nc.vector.tensor_copy, 2, H, M)
         quantize(2, 0, M)
         multiply_dw(2, 0)
         multiply_dw(2, 1)

from contextlib import ExitStack

import concourse.mybir as mybir
from concourse.masks import make_identity

K, M, T, S = 2048, 256, 512, 256
FLOPS = 2 * 2 * K * M * S

F32 = mybir.dt.float32
BF16 = mybir.dt.bfloat16
I32 = mybir.dt.int32
U32 = mybir.dt.uint32
U16 = mybir.dt.uint16
U8 = mybir.dt.uint8
E4M3X4 = mybir.dt.float8_e4m3fn_x4
E2M1X4 = mybir.dt.float4_e2m1fn_x4
GELU = mybir.ActivationFunctionType.Gelu_apprx_tanh
ADD = mybir.AluOpType.add

P = 128
PASSES = K // 512
H = 128


def tile_list_tabd_tm_gelu_kernel(tc, tab, w4_words, w4_scales, dw, b, offs, out):
    nc = tc.nc
    with ExitStack() as ctx:
        keep = ctx.enter_context(tc.tile_pool(name="keep", bufs=1))
        psum = ctx.enter_context(tc.psum_pool(name="psum", bufs=1))

        offsets = keep.tile([P, S // 16], U16, name="offsets")
        words = [keep.tile([P, T], I32, name=f"words{a}", align_bytes=64) for a in range(PASSES)]
        table_scales = keep.tile([P, PASSES * T], U8, name="table_scales", align_bytes=64)
        w4_codes = keep.tile([P, PASSES, 2 * M], U8, name="w4_codes", align_bytes=64)
        w4_scale = keep.tile([P, PASSES * M], U8, name="w4_scale", align_bytes=64)
        picked_words = [keep.tile([P, S], U32, name=f"picked_words{a}", align_bytes=64) for a in range(PASSES)]
        picked_scales = [keep.tile([P, S], U8, name=f"picked_scales{a}", align_bytes=64) for a in range(PASSES)]
        parts = [(a, 0, 4) for a in range(PASSES - 1)] + [(PASSES - 1, 0, 2), (PASSES - 1, 2, 2)]
        raw = [keep.tile([P, rows, M], F32, name=f"raw{i}", align_bytes=64) for i, (a, t, rows) in enumerate(parts)]
        grouped = [keep.tile([P, 4 * M], BF16, name=f"grouped{a}", align_bytes=64) for a in range(PASSES)]
        dw_codes = [keep.tile([P, M], U32, name=f"dw_codes{a}", align_bytes=64) for a in range(PASSES)]
        dw_scales = [keep.tile([P, M], U8, name=f"dw_scales{a}", align_bytes=64) for a in range(PASSES)]
        bias_rows = keep.tile([P, P], F32, name="bias_rows", align_bytes=64)
        bias_cols = keep.tile([P, 2], F32, name="bias_cols")
        identity = keep.tile([P, P], F32, name="identity", align_bytes=64)
        bias = keep.tile([P, M], F32, name="bias", align_bytes=64)
        dummy = keep.tile([P, 1], F32, name="dummy")

        bias_cols_psum = psum.tile([P, P], F32, name="bias_cols_psum")
        bias_psum = psum.tile([P, M], F32, name="bias_psum")
        acc = {(j, h): psum.tile([P, H], F32, name=f"acc{j}{h}") for h in range(2) for j in range(2)}

        tab32 = tab.bitcast(I32)
        table_words = T * P
        tab_scale_rows = tab32[:, table_words:].rearrange("a (q r t) -> r q a t", q=4, r=4)
        w4_scale_rows = w4_scales.bitcast(I32).rearrange("a (q r) n -> r q a n", q=4)

        def load_words(a):
            nc.sync.dma_start(words[a][:], tab32[a, 0:table_words].rearrange("(p t) -> p t", p=P))

        def load_dw(i):
            a, t, rows = parts[i]
            nc.sync.dma_start(
                raw[i][:], dw[512 * a : 512 * (a + 1), :].rearrange("(p j) n -> p j n", j=4)[:, t : t + rows, :]
            )

        nc.gpsimd.memset(table_scales[:].bitcast(I32), 0)
        nc.vector.memset(bias_rows[:], 0.0)
        nc.vector.memset(dummy[:], 0.0)
        nc.vector.memset(w4_scale[:].bitcast(I32), 0)
        nc.scalar.activation(dummy[:], dummy[:], GELU)

        nc.gpsimd.dma_start(bias_rows[0:2, :], b.rearrange("(h n) -> h n", h=2))
        make_identity(nc, identity[:])
        nc.sync.dma_start(offsets[:], offs)
        load_words(0)
        load_words(1)
        for r in range(4):
            nc.sync.dma_start(
                table_scales[r:P:32, :].bitcast(I32).rearrange("q (a t) -> q a t", a=PASSES), tab_scale_rows[r]
            )
        load_dw(0)
        load_dw(1)
        load_words(2)
        nc.sync.dma_start(w4_codes[:].bitcast(I32), w4_words.bitcast(I32).rearrange("a p n -> p a n"))
        for r in range(4):
            nc.sync.dma_start(
                w4_scale[r:P:32, :].bitcast(I32).rearrange("q (a n) -> q a n", a=PASSES), w4_scale_rows[r]
            )
        load_words(3)
        load_dw(2)
        load_dw(3)
        load_dw(4)

        def gather_words(a):
            nc.vector.tensor_copy(picked_words[a][:], words[a][:].bitcast(U32).indirect(offsets[:]))

        def gather_scales(a):
            nc.vector.tensor_copy(picked_scales[a][:], table_scales[:, a * T : (a + 1) * T].indirect(offsets[:]))

        def interleave(copy, i, c0, c1):
            a, t, rows = parts[i]
            dst = grouped[a][:, 4 * c0 : 4 * c1].rearrange("p (c i t) -> p c t i", i=4, t=4)[:, :, t : t + rows, :]
            copy(dst, raw[i][:, :, c0:c1].rearrange("p t (c i) -> p c t i", i=4))

        def quantize(a, c0, c1):
            nc.vector.quantize_mx(
                out=dw_codes[a][:, c0:c1].bitcast(E4M3X4),
                scales=dw_scales[a][:, c0:c1],
                in_=grouped[a][:, 4 * c0 : 4 * c1],
            )

        def table_operand(a, j):
            cols = slice(j * H, (j + 1) * H)
            return dict(lhsT=picked_words[a][:, cols].bitcast(E4M3X4), lhsT_scale=picked_scales[a][:, cols])

        def multiply_w4(a):
            for h in range(2):
                for j in range(2):
                    nc.tensor.matmul_mx(
                        out=acc[j, h][:],
                        **table_operand(a, j),
                        rhs=w4_codes[:, a, 2 * H * h : 2 * H * (h + 1)].bitcast(E2M1X4),
                        rhs_scale=w4_scale[:, a * M + H * h : a * M + H * (h + 1)],
                        start=False,
                        stop=False,
                    )

        def multiply_dw(a, h):
            cols = slice(H * h, H * (h + 1))
            for j in range(2):
                nc.tensor.matmul_mx(
                    out=acc[j, h][:],
                    **table_operand(a, j),
                    rhs=dw_codes[a][:, cols].bitcast(E4M3X4),
                    rhs_scale=dw_scales[a][:, cols],
                    start=(a == 0),
                    stop=(a == PASSES - 1),
                )

        def finish(h):
            cols = slice(h * H, (h + 1) * H)
            for j in range(2):
                biased = keep.tile([P, H], F32, name=f"biased{j}{h}", align_bytes=64)
                result = keep.tile([P, H], F32, name=f"result{j}{h}", align_bytes=64)
                nc.vector.tensor_tensor(biased[:], acc[j, h][:], bias[:, cols], ADD)
                nc.scalar.activation(result[:], biased[:], GELU)
                nc.sync.dma_start(out[j * H : (j + 1) * H, cols], result[:])

        nc.tensor.transpose(bias_cols_psum[:], bias_rows[:], identity[:])
        nc.scalar.copy(bias_cols[:], bias_cols_psum[:, 0:2])
        for h in range(2):
            nc.tensor.transpose(
                bias_psum[:, h * P : (h + 1) * P], bias_cols[:, h : h + 1].to_broadcast([P, P]), identity[:]
            )
        nc.scalar.copy(bias[:], bias_psum[:])

        gather_words(0)
        gather_words(1)
        gather_scales(0)
        gather_scales(1)
        interleave(nc.scalar.copy, 0, 0, M)
        quantize(0, 0, M)
        multiply_dw(0, 0)
        multiply_dw(0, 1)
        multiply_w4(0)
        multiply_w4(1)
        gather_words(2)
        gather_scales(2)
        interleave(nc.scalar.copy, 1, 0, M)
        quantize(1, 0, M)
        multiply_dw(1, 0)
        multiply_dw(1, 1)
        multiply_w4(2)
        gather_words(3)
        gather_scales(3)
        interleave(nc.scalar.copy, 2, 0, H)
        interleave(nc.vector.tensor_copy, 2, H, M)
        quantize(2, 0, M)
        multiply_dw(2, 0)
        multiply_dw(2, 1)
        multiply_w4(3)
        interleave(nc.scalar.copy, 3, 0, M)
        interleave(nc.scalar.copy, 4, 0, H)
        interleave(nc.vector.tensor_copy, 4, H, M)
        quantize(3, 0, H)
        multiply_dw(3, 0)
        quantize(3, H, M)
        multiply_dw(3, 1)
        finish(0)
        finish(1)
